import numpy as np, ml_dtypes
CORES = [23,119,17,113]
N = 4
BF = ml_dtypes.bfloat16
def gentries(a):
    return np.ascontiguousarray(a.reshape(8, 16, -1).transpose(0, 2, 1)).reshape(8, -1)
def gtable(e):
    e = np.asarray(e); return np.ascontiguousarray(e.reshape(8, -1, 16).transpose(0, 2, 1)).reshape(128, -1).astype(np.int32)
NO, D, B, K, RO, TH = 16, 3, 224, 16, 4, 9
V, NB = NO * B, NO + D
def every(z):
    return np.concatenate([z, np.stack([np.roll(z[:, :, d - 1], d, axis=0) for d in range(1, D + 1)], axis=2)], axis=2)
def parts(rng):
    a = rng.integers(0, 256, (N, 8, 15, V)); m = (rng.random((N, 8, V)) < 0.0625).astype(np.int64)
    u = np.argsort(rng.random((N, 8, NB, V)), axis=-1)[..., :16 * B].reshape(N, 8, NB, 16, B)
    e = np.argsort(rng.random((N, 8, NO, B)), axis=-1)[..., :K]
    return a, m, u, np.ascontiguousarray(e)
def firsts(e):
    z = np.zeros((N, 8, V), bool); np.put_along_axis(z, (e + B * np.arange(NO)[:, None]).reshape(N, 8, -1), True, 2)
    return z
def reach(u, e):
    z = np.zeros((N, 8, V), bool); q = np.take_along_axis(u, every(e)[:, :, :, None, :], 4)
    np.put_along_axis(z, q.reshape(N, 8, -1), True, 2)
    return z
def cover(rng):
    o = np.argsort(rng.random((N, V)), axis=-1)
    return np.stack([np.roll(o, -16 * K * c, axis=1) for c in range(NB)], axis=1)
def aim(rng, e, g, o):
    ee = every(e)[:, g]; w = np.zeros((N, NB, 16, B), np.int64)
    for r in range(N):
        for c in range(NB):
            rest = np.ones(B, bool); rest[ee[r, c]] = False
            w[r, c][:, ee[r, c]] = o[r, c, :16 * K].reshape(16, K)
            w[r, c][:, rest] = rng.permutation(o[r, c, 16 * K:])[:16 * (B - K)].reshape(16, B - K)
    return w
def pack(a, m, u, e):
    rec = np.concatenate([a, m[:, :, None]], axis=2).reshape(N, 128, V).astype(np.float32).astype(BF)
    up = np.ascontiguousarray(u.transpose(0, 1, 3, 2, 4).reshape(N, 128, NB * B)).astype(np.int32)
    return {"rec": rec, "up": up, "fr": np.stack([gtable(z.reshape(8, -1)) for z in e])}
def setup_inputs(rng):
    return pack(*parts(rng))
def setup_inputs_room(rng):
    a, m, u, e = parts(rng); c = reach(u, e); z = firsts(e); can = c & ~z; pick = np.zeros((N, 8, V), bool)
    for r in range(N):
        for g in range(8):
            for b in range(NO):
                o = b * B + rng.permutation(np.flatnonzero(can[r, g, b * B:(b + 1) * B])); n = int(rng.choice(np.array([0, 1, K - 1, K, K + 1, B])))
                if r == 0 and b == 0: n = (K, K + 1, B, K - 1, 1, 0, K, K + 1)[g]
                pick[r, g, o[:n]] = True
    a = np.where(c[:, :, None], np.where(pick[:, :, None], rng.integers(150, 256, a.shape), rng.integers(0, 51, a.shape)), a)
    a = np.where(z[:, :, None], rng.integers(100, 111, a.shape), a)
    return pack(a, z.astype(np.int64), u, e)
def setup_inputs_ties(rng):
    a, m, u, e = parts(rng); z = firsts(e)
    lo = np.array([0, 254, 100, 0, 7, 127, 1, 128]).reshape(1, 8, 1, 1); step = np.array([1, 1, 1, 255, 1, 1, 2, 1]).reshape(1, 8, 1, 1)
    p = np.where(z, 0.6, 0.15 + 0.3 * rng.random((N, 8, V)))[:, :, None]
    a = lo + step * (rng.random(a.shape) < p)
    a[:, 1] = np.where((rng.random((N, V)) < 0.6)[:, None], 255, a[:, 1])
    return pack(a, m, u, e)
def setup_inputs_meet(rng):
    a, m, u, e = parts(rng)
    u[:, ::2] = u[:, ::2, :1].copy(); e[:, ::2] = e[:1, ::2, :1].copy()
    i = 1 + np.argsort(rng.random((N, 4, NO, B - 2)), axis=-1)[..., :K - 2]
    e[:, 1::2, :, 2:] = i; e[:, 1::2, :, 0] = 0; e[:, 1::2, :, 1] = B - 1
    base = np.arange(16 * B).reshape(B, 16).T; u[:, 1] = base; u[:, 1, NO:] = base + V - 16 * B
    o = np.argsort((np.arange(V) + rng.integers(0, 16, (N, 1, 1))) % 16 + rng.random((N, 1, V)), axis=-1)
    u[:, 2] = aim(rng, e, 2, np.broadcast_to(o, (N, NB, V)))[:, :1]
    u[:, 3] = aim(rng, e, 3, cover(rng)); z = firsts(e)
    a[:, 3] = np.where(z[:, 3][:, None], rng.integers(0, 51, (N, 15, V)), rng.integers(150, 256, (N, 15, V))); m[:, 3] = 0
    return pack(a, m, u, e)
def setup_inputs_dry(rng):
    a, m, u, e = parts(rng); z = firsts(e); o = rng.permutation(8)
    a[:, o[1]] = np.where(z[:, o[1]][:, None], rng.integers(100, 256, (N, 15, V)), rng.integers(0, 100, (N, 15, V)))
    for g in (o[3], o[4]):
        a[:, g] = np.where(rng.random((N, 15, V)) < 0.7, 255, rng.integers(0, 101, (N, 15, V)))
    a[:, o[3], :, ::B] = 0
    u[:, o[5]] = aim(rng, e, o[5], cover(rng))
    a[:, o[5]] = np.where(z[:, o[5]][:, None], rng.integers(0, 31, (N, 15, V)), rng.integers(80, 256, (N, 15, V)))
    a[:, o[5], :, ::B] = rng.integers(60, 101, (N, 15, NO))
    m[:, o[0]] = 1; m[:, o[2]] = rng.random((N, V)) < 0.9; m[:, o[3]] = 1; m[:, o[4]] = rng.random((N, V)) < 0.95
    m[:, o[5]] = 1; m[:, o[5], ::B] = 0
    m[(rng.integers(-2, 1) + np.arange(3)) % N] = 1
    return pack(a, m, u, e)
def setup_inputs_spread(rng):
    a, m, u, e = parts(rng); s = np.exp2(8.2 * rng.random((N, 8, 1, V)))
    a = np.minimum((s * rng.random(a.shape)).astype(np.int64), 255); m = (rng.random(m.shape) < rng.random((N, 8, 1)) * 0.5).astype(np.int64)
    return pack(a, m, u, e)
def check_inputs(d):
    bad = []
    r = d["rec"].astype(np.float32).reshape(N, 8, 16, V); a, m = r[:, :, :15], r[:, :, 15]
    if not np.all((a >= 0) & (a <= 255) & (a == np.floor(a))): bad.append("notes in rec")
    if not np.all((m == 0) | (m == 1)): bad.append("marks in rec")
    if np.min(d["up"]) < 0 or np.max(d["up"]) > V - 1: bad.append("range of up")
    u = np.sort(d["up"].reshape(N, 8, 16, NB, B).transpose(0, 1, 3, 2, 4).reshape(N, 8, NB, 16 * B), axis=-1)
    if np.any(u[..., 1:] == u[..., :-1]): bad.append("different parents in a bank of up")
    if np.min(d["fr"]) < 0 or np.max(d["fr"]) > B - 1: bad.append("range of fr")
    e = np.sort(np.stack([gentries(z) for z in d["fr"]]).reshape(N, 8, NO, K), axis=-1)
    if np.any(e[..., 1:] == e[..., :-1]): bad.append("different places in a bank of fr")
    return bad
def reference(rec, up, fr):
    s = rec.astype(np.float32).astype(np.int64).reshape(N, 8, 16, V); a = s[:, :, :15].copy(); mark = s[:, :, 15] > 0
    u = up.astype(np.int64).reshape(N, 8, 16, NB, B)
    e = np.stack([gentries(z) for z in fr]).astype(np.int64).reshape(N, 8, NO, K); live = np.ones(e.shape, bool)
    for wave in range(RO):
        node = e + B * np.arange(NO)[:, None]
        x = np.take_along_axis(a, node.reshape(N, 8, 1, NO * K), 3).reshape(N, 8, 15, NO, K)
        ee, ll, xx = every(e), every(live), every(np.moveaxis(x, 2, 3))
        new = a.copy(); hit = np.zeros((N, 8, V), bool)
        for b in range(NB):
            q = np.take_along_axis(u[:, :, :, b], ee[:, :, None, b], 3).reshape(N, 8, 1, 16 * K)
            old = np.take_along_axis(a, q, 3)
            arr = np.tile(xx[:, :, b], (1, 1, 1, 16))
            ok = (np.add.reduce((old >= arr).astype(np.int64), axis=2) >= TH) & np.tile(ll[:, :, b], (1, 1, 16))
            r, g, j = np.nonzero(ok); to = q[r, g, 0, j]
            new[r, g, :, to] = ((old + arr) >> 1)[r, g, :, j]
            hit[r, g, to] = True
        h = (hit & ~mark).reshape(N, 8, NO, B); mark = mark | hit; a = new
        e = np.argsort(~h, axis=-1, kind="stable")[..., :K]; live = np.take_along_axis(h, e, 3)
    return {"y": np.concatenate([a, mark[:, :, None].astype(np.int64)], axis=2).reshape(N, 128, V).astype(np.float32).astype(BF)}

from concourse.bass import DstId, RemoteDMATransfer
from concourse.mybir import AluOpType, AxisListType, ActivationFunctionType

OP, ACT = AluOpType, ActivationFunctionType
N, B, NO, NB, D, WAVES = 4, 224, 16, 19, 3, 4
V = NO * B
S = 240
W0 = V + 384
OFF = 4096
WT = OFF + W0
PW = 17
BIG = 8388608.0
BLOCKS = [(0, 4), (4, 8), (8, 12), (12, 16), (16, 19)]
LISTS = [(0, 4), (4, 8), (8, 16)]
GATHER = "avaaa"
CMP = "aaaavvaaaa"
VAL = "vaaaaaaaaa"
CNT = "vvaaaava"
XG = "vaa"
XEV = "aaaaa"
INIT = 1792

SCRATCH = {}
for _n, _w, _d in (("fr_s", 16, "int32"), ("rb", W0, "bfloat16"), ("a0", WT, "float32"), ("a1", WT, "float32"), ("up_s", NB * S, "int32"),
                   ("dm", 16, "int32"), ("kI", 8, "int32"), ("kc", 8, "float32"), ("E", 1024, "bfloat16"), ("EG", 768, "bfloat16"),
                   ("HI", 128, "bfloat16"), ("NI", 128, "bfloat16"), ("WS", 144, "bfloat16"), ("RM", 2048, "bfloat16"),
                   ("XT", 128 * 8, "bfloat16"), ("TU", 16, "float32"), ("TN", 16, "float32"), ("TG", 8, "float32"), ("f0", 256, "bfloat16"),
                   ("f1", 256, "float32"), ("f2", 256, "float32"), ("f3", 256, "float32"), ("rk", S, "bfloat16"), ("junk", NO * S, "bfloat16"),
                   ("sums", 16, "float32"), ("tu", 32, "float32"), ("tn", 32, "float32"), ("lu", 32, "uint16"), ("ln", 32, "uint16"),
                   ("q16", 16 * NB, "uint16"), ("qs", 16 * NB, "float32"), ("x", 16 * NO, "bfloat16"), ("old", 256 * NB, "bfloat16"),
                   ("cb", 256 * NB, "bfloat16"), ("val", 256 * NB, "float32"), ("of", 16 * NB, "float32"), ("o16", 16 * NB, "uint16"),
                   ("yb", V, "bfloat16")):
    SCRATCH[_n] = ("sbuf", [128, _w], _d)
for _i in range(WAVES):
    SCRATCH["snd%d" % _i] = ("sbuf", [128, D * PW], "bfloat16")
    SCRATCH["rcv%d" % _i] = ("sbuf", [128, D * PW], "bfloat16")
PSUM = ["p0", "p1", "p2", "p3", "r0", "r1", "px", "pc"]
for _n in PSUM:
    SCRATCH[_n] = ("psum", [128, 512], "float32")
SEMAPHORES = ["sv", "sa", "sp", "sg", "sent"] + ["gh%d" % i for i in range(WAVES)] + ["d%d" % i for i in range(40)]

SEED, NOISE = 660, 0.0
CYC = 1e-3
GA, SC, PECYC, HOP, LAT, BW, DLAT, EPS = 1.5, 2.0, 0.7e-3, 0.12, 10.0, 200e3, 1.8, 0.1


def R(buf, lo, hi, step=1, p0=0, p1=128):
    return (buf, lo, hi, step, p0, p1)


def ap(T, r):
    if r[0] == "at":
        return ap(T, r[1]).indirect(ap(T, r[2]))
    b, lo, hi, step, p0, p1 = r
    return T[b][p0:p1, lo:hi] if step == 1 else T[b][p0:p1, lo:hi:step]


def width(r):
    return 16 * width(r[2]) if r[0] == "at" else -(-(r[2] - r[1]) // r[3])


def plan():
    ops, hist = [], {}

    def access(i, r, kind):
        if r[0] == "at":
            access(i, r[1], kind)
            access(i, r[2], "r")
            return
        buf, lo, hi = r[0], r[1], r[2]
        deps, psum = ops[i]["deps"], buf in PSUM
        if psum:
            lo, hi = 0, 512
        keep = []
        for (l, h, j, k) in hist.get(buf, []):
            if j != i and l < hi and lo < h and (psum or kind == "w" or k == "w"):
                a, b = ops[j], ops[i]
                if a["q"] == "p" and b["q"] == "p":
                    deps.setdefault(j, False)
                else:
                    deps[j] = deps.get(j, False) or k == "w" or a["dma"] > 0 or b["dma"] > 0 or a["q"] != b["q"]
            if not (lo <= l and h <= hi and kind == "w" and j != i):
                keep.append((l, h, j, k))
        hist[buf] = keep + [(lo, hi, i, kind)]

    def add(q, fn, reads, writes, cost, dma=0, lat=0.0):
        ops.append({"q": q, "fn": fn, "cost": cost, "dma": dma, "lat": lat, "deps": {}})
        for r in reads:
            access(len(ops) - 1, r, "r")
        for r in writes:
            access(len(ops) - 1, r, "w")

    def cy(out, in_, k=1.0):
        k = SC if out[0] == "at" else (GA if in_[0] == "at" else k)
        return 0.055 + max(64, width(in_) * k) * CYC

    def load(q, out, name, rows, lo, hi, size):
        add(q, lambda g, T: (g.sync if q == "s" else g.scalar).dma_start(ap(T, out), T[name][rows, lo:hi]), [], [out], 0.06, size)

    def move(out, in_, size):
        add("s", lambda g, T: g.sync.dma_start(ap(T, out), ap(T, in_)), [in_], [out], 0.06, size)

    def fill(r, x):
        add("v", lambda g, T: g.vector.memset(ap(T, r), x), [], [r], cy(r, r, 0.5))

    def copy(q, out, in_, bias=0.0):
        if q == "v":
            add("v", lambda g, T: g.vector.tensor_copy(ap(T, out), ap(T, in_)), [in_], [out], cy(out, in_))
        else:
            add("a", lambda g, T: g.scalar.activation(ap(T, out), ap(T, in_), ACT.Copy, bias=bias), [in_], [out], cy(out, in_))

    def scal(out, in_, a, b, o0, o1=None):
        reads = [in_] + ([a] if isinstance(a, tuple) else [])
        if o1 is None:
            add("v", lambda g, T: g.vector.tensor_scalar(ap(T, out), ap(T, in_), ap(T, a) if isinstance(a, tuple) else a, None, o0), reads, [out], cy(out, in_))
        else:
            add("v", lambda g, T: g.vector.tensor_scalar(ap(T, out), ap(T, in_), ap(T, a) if isinstance(a, tuple) else a, b, o0, o1), reads, [out], cy(out, in_))

    def both(out, x, y, op, k=2.0):
        add("v", lambda g, T: g.vector.tensor_tensor(ap(T, out), ap(T, x), ap(T, y), op), [x, y], [out], cy(out, x, k))

    def sign(out, in_, bias, scale, acc=None):
        reads = [in_] + ([bias] if isinstance(bias, tuple) else [])
        add("a", lambda g, T: g.scalar.activation(ap(T, out), ap(T, in_), ACT.Sign, bias=ap(T, bias) if isinstance(bias, tuple) else bias, scale=scale,
                                                  accum_out=ap(T, acc) if acc else None), reads, [out] + ([acc] if acc else []), cy(out, in_) + 0.02)

    def mm(out, lhs, rhs, start, stop):
        add("p", lambda g, T: g.tensor.matmul(ap(T, out), ap(T, lhs), ap(T, rhs), start, stop), [lhs, rhs], [out], 0.03 + max(64, width(rhs)) * PECYC)

    def pick(r, pat, op, x, base, cm):
        add("g", lambda g, T: g.affine_select(ap(T, r), ap(T, r), pat, op, x, base, cm), [r], [r], 0.17 + 2 * CYC * width(r))

    def iota(r, pat, base, cm):
        add("g", lambda g, T: g.iota(ap(T, r), pat, base, cm, allow_small_or_imprecise_dtypes=True), [], [r], 0.13 + 2 * CYC * width(r))

    every = slice(0, 128)
    load("s", R("fr_s", 0, 16), "fr", every, 0, 16, 8192)
    load("s", R("rb", 0, V), "rec", every, 0, V, 256 * V)
    for b in range(NB):
        load("sa"[b % 2], R("up_s", b * S, b * S + B), "up", every, b * B, b * B + B, 512 * B)
    load("s", R("f0", 0, B), "rec", slice(15, 128, 16), 0, V, 57344)

    fill(R("rb", V, W0), 0.0)
    iota(R("dm", 0, 16), [[16, 16]], V, 1)
    for (tb, st) in (("TU", 2 * S), ("TN", 2 * B)):
        if "v" in CNT:
            iota(R(tb, 0, 16), [[st, 16]], 0, 0)
        for p in range(8):
            if CNT[p] == "a" and (p == 0 or CNT[p - 1] != "a"):
                e = p
                while e < 8 and CNT[e] == "a":
                    e += 1
                iota(R(tb, 2 * p, 2 * e), [[st, 2 * (e - p)]], 2 * p * st + S, 0)
    fill(R("HI", 0, 128), 0.5)
    pick(R("HI", 0, 128), [[-1, 128]], OP.is_equal, 0.0, 0, 1)
    pick(R("HI", 0, 128), [[0, 8], [1, 16]], OP.not_equal, 0.0, -15, 0)
    fill(R("E", 0, 1024), 1.0)
    pick(R("E", 0, 1024, 1, 0, 64), [[1, 1024]], OP.is_ge, 0.0, 0, -16)
    pick(R("E", 0, 1024, 1, 0, 64), [[-1, 1024]], OP.is_ge, 0.0, 15, 16)
    scal(R("NI", 0, 128), R("HI", 0, 128), -1.0, None, OP.mult)
    NX = 128 * len(BLOCKS)
    fill(R("XT", 0, NX), -0.25)
    pick(R("XT", 0, NX), [[0, NX // 16], [1, 16]], OP.not_equal, 1.0, -15, 0)
    fill(R("XT", 0, NX, 1, 0, 64), 0.0)
    fill(R("WS", 0, 144), 1.0)
    pick(R("WS", 0, 144), [[0, 9], [1, 16]], OP.is_equal, 0.0, -15, 0)
    pick(R("WS", 0, 144), [[-16, 9], [0, 16]], OP.is_ge, 0.0, 0, 1)
    pick(R("WS", 0, 144), [[16, 9], [0, 16]], OP.is_ge, 0.0, 14, -1)
    iota(R("TG", 0, D), [[S, D]], S * NO, 0)
    fill(R("EG", 0, 768), 1.0)
    pick(R("EG", 0, 768, 1, 0, 64), [[16 * PW, D], [1, 256]], OP.is_ge, 0.0, 0, -16)
    pick(R("EG", 0, 768, 1, 0, 64), [[-16 * PW, D], [-1, 256]], OP.is_ge, 0.0, 15, 16)
    fill(R("RM", 0, 2048), 1.0)
    pick(R("RM", 0, 2048), [[-1, 16], [-16, 8], [0, 16]], OP.is_equal, 0.0, 0, 1)
    iota(R("kI", 0, 1), [[0, 1]], 0, 1)
    scal(R("kI", 1, 2), R("kI", 0, 1), 15, None, OP.bitwise_and)
    copy("v", R("kc", 0, 1), R("kI", 1, 2))
    scal(R("kc", 1, 2), R("kI", 1, 2), 0.5, None, OP.add)
    for b in range(NB):
        copy("v", R("up_s", b * S + B, b * S + S), R("dm", 0, 16))
    fill(R("a0", OFF + V, WT), 0.0)
    copy("v", R("a0", OFF, OFF + INIT), R("rb", 0, INIT))
    copy("a", R("a0", OFF + INIT, OFF + V), R("rb", INIT, V))
    for w in range(WAVES):
        fill(R("f%d" % w, B, S), float(w))
    fill(R("a1", OFF + V, WT), 0.0)
    rot = {"p": 0, "r": 0}

    def tile(kind, n):
        rot[kind] += 1
        return kind + str((rot[kind] - 1) % n)

    def wave(w):
        src = R("rb", 0, W0) if w == 0 else R("a%d" % ((w - 1) % 2), OFF, WT)
        dst, snd, rcv = "a%d" % (w % 2), "snd%d" % w, "rcv%d" % w
        if w == 0:
            for p in range(8):
                c = (2 * p, 2 * p + 2)
                if CNT[p] == "a":
                    scal(R("sums", *c), R("fr_s", *c), 2.0, float(-S), OP.mult, OP.add)
                else:
                    scal(R("sums", *c), R("fr_s", *c), 2.0, None, OP.mult)
        else:
            fn, fo = R("f%d" % w, 0, S), R("f%d" % (w - 1), 0, S)
            add("v", lambda g, T: g.vector.tensor_tensor_scan(T.rk[:, :], ap(T, fn), ap(T, fo), 0.0, OP.add, OP.subtract), [fn, fo], [R("rk", 0, S)], 0.3)
            for p in range(8):
                t = tile("r", 2)
                for h in range(2):
                    b = 2 * p + h
                    mm(R(t, h * S, h * S + S), R("RM", b * 128, b * 128 + 128), R("rk", 0, S), True, True)
                if CNT[p] == "v":
                    scal(R("junk", 2 * p * S, 2 * p * S + 2 * S), R(t, 0, 2 * S), R("kc", 0, 1), 2.0, OP.is_le, OP.mult)
                for h in range(2):
                    b = 2 * p + h
                    jk, sm = R("junk", b * S, b * S + S), R("sums", b, b + 1)
                    if CNT[p] == "a":
                        sign(jk, R(t, h * S, h * S + S), R("kc", 1, 2), -1.0, sm)
                    else:
                        add("v", lambda g, T, jk=jk, sm=sm: g.vector.tensor_reduce(ap(T, sm), ap(T, jk), AxisListType.X, OP.add), [jk], [sm], 0.3)

        def lists(lo, hi, xq):
            for (tm, tb, ls) in (("tu", "TU", "lu"), ("tn", "TN", "ln")):
                both(R(tm, lo, hi), R("sums", lo, hi), R(tb, lo, hi), OP.add)
                scal(R(ls, lo, hi), R(tm, lo, hi), 0.5, None, OP.mult)
            q = R("q16", lo * 16, hi * 16)
            copy("v", q, ("at", R("up_s", 0, hi * S), R("lu", lo, hi)))
            copy(xq, R("x", lo * 16, hi * 16), ("at", src, R("ln", lo, hi)))
            scal(R("qs", lo * 16, hi * 16), q, 64.0, None, OP.add)

        def block(k, m, buf, lo):
            mm(R("px", 0, 128, 1, 0, m), R(buf, lo, lo + m), R("HI", 0, 128), True, True)
            copy(XEV[k], R("XT", k * 128, k * 128 + 128, 1, 0, m), R("px", 0, 128, 1, 0, m))

        def unit(u):
            k, (b0, b1) = u, BLOCKS[u]
            lo, hi, n = b0 * 256, b1 * 256, 16 * (b1 - b0)
            l16, h16 = b0 * 16, b1 * 16
            copy(GATHER[u], R("old", lo, hi), ("at", src, R("q16", l16, h16)))
            for b in range(b0, b1, 2):
                a, z = b * 256, min(b + 2, b1) * 256
                m, eo = z - a, (b - b0) * 256
                od, cq = R("old", a, z), CMP[b // 2]
                xt, ex = R("XT", k * 128, k * 128 + 128, 1, 0, 65), R("EG" if b0 == NO else "E", eo, eo + m, 1, 0, 65)
                if cq == "a":
                    t = R(tile("p", 4), 0, m)
                    mm(t, xt, ex, True, False)
                    mm(t, R("NI", 0, 128), od, False, True)
                    sign(R("cb", a, z), t, 0.0, -1.0)
                t = R(tile("p", 4), 0, m)
                mm(t, xt, ex, True, False)
                mm(t, R("HI", 0, 128), od, False, True)
                if cq == "v":
                    both(R("cb", a, z), od, t, OP.is_gt, 1.0)
                if VAL[b // 2] == "a":
                    copy("a", R("val", a, z), t, BIG)
                else:
                    scal(R("val", a, z), t, BIG, None, OP.add)

            def count(g, T):
                for i in range(16):
                    r = g.tensor.matmul(T.pc[:, 0:n], T.WS[:, 15 - i:143 - i], T.cb[:, lo + i:hi:16], i == 0, i == 15)
                return r
            add("p", count, [R("cb", lo, hi), R("WS", 0, 144)], [R("pc", 0, n)], 16 * (0.01 + max(64, n) * PECYC))
            sign(R("pc", 256, 256 + n), R("pc", 0, n), -2.0 if CMP[b0 // 2] == "a" else -8.5, 1.0)
            both(R("of", l16, h16), R("pc", 256, 256 + n), R("qs", l16, h16), OP.mult, 1.0)
            scal(R("o16", l16, h16), R("of", l16, h16), float(OFF - 64), None, OP.add)
            for b in range(b0, b1):
                scal(("at", R(dst, 0, WT), R("o16", b * 16, b * 16 + 16)), R("val", b * 256, b * 256 + 256), 1.0, -BIG, OP.mult, OP.add)

        done = 0
        for (li, (lo, hi)) in enumerate(LISTS):
            lists(lo, hi, XG[li])
            if lo < D <= hi:
                for (l, h) in ((0, 2), (2, D)):
                    scal(R(snd, l * PW + 16, h * PW, PW), R("sums", l, h), 0.5, (S / 2 if CNT[l // 2] == "a" else 0.0), OP.mult, OP.add)
                for d in range(D):
                    o, i = R(snd, d * PW, d * PW + 16), R("x", d * 16, d * 16 + 16)
                    add("g", lambda g, T, o=o, i=i: g.affine_select(ap(T, o), ap(T, i), [[0, 16]], OP.is_equal, 0.0, 0, 0), [i], [o], 0.2)
                add("g", w, [R(snd, 0, D * PW)], [R(rcv, 0, D * PW)], 1.5, 0, LAT)
            while BLOCKS[done][1] <= hi:
                block(done, 16 * (BLOCKS[done][1] - BLOCKS[done][0]), "x", BLOCKS[done][0] * 16)
                unit(done)
                done += 1
        both(R("tu", 16, 16 + D), R(rcv, 16, D * PW, PW), R("TG", 0, D), OP.add)
        copy("v", R("lu", 16, 16 + D), R("tu", 16, 16 + D))
        copy("v", R("q16", 256, 304), ("at", R("up_s", 0, NB * S), R("lu", 16, 16 + D)))
        scal(R("qs", 256, 304), R("q16", 256, 304), 64.0, None, OP.add)
        block(done, D * PW, rcv, 0)
        unit(done)
        if w < WAVES - 1:
            o = R("f%d" % (w + 1), 0, B)
            add("s", lambda g, T: g.sync.dma_start(ap(T, o), T[dst][15::16, OFF:OFF + V]), [R(dst, OFF, OFF + V)], [o], 0.06, 114688)
            move(R("a%d" % ((w + 1) % 2), OFF, OFF + V), R(dst, OFF, OFF + V), 512 * V)
            ops[-1]["deps"].setdefault(len(ops) - 2, False)
        else:
            for j in range(4):
                lo, hi = j * (V // 4), (j + 1) * (V // 4)
                o = R("yb", lo, hi)
                copy("va"[j % 2], o, R(dst, OFF + lo, OFF + hi))
                add("s", lambda g, T, o=o: g.sync.dma_start(T.y[:, o[1]:o[2]], ap(T, o)), [o], [], 0.06, 64 * V)

    for w in range(WAVES):
        wave(w)
    return ops


def order(ops):
    n = len(ops)
    succ, need = [[] for _ in ops], [len(o["deps"]) for o in ops]
    for i, o in enumerate(ops):
        for j in o["deps"]:
            succ[j].append(i)
    bl, rs = [0.0] * n, SEED
    for i in range(n - 1, -1, -1):
        o = ops[i]
        rs = (rs * 1103515245 + 12345) % 2147483648
        bl[i] = (rs / 2147483648.0 - 0.5) * NOISE + o["cost"] + o["lat"] + (DLAT + o["dma"] / BW if o["dma"] else 0.0) + max([bl[j] + HOP for j in succ[i]] + [0.0])
    free, dma, rt = {q: 0.0 for q in "vapgs"}, 0.0, [0.0] * n
    ready = {q: [i for i in range(n) if need[i] == 0 and ops[i]["q"] == q] for q in "vapgs"}
    out = []
    while len(out) < n:
        e, q = min((min(max(free[q], rt[i]) for i in ready[q]), q) for q in "vapgs" if ready[q])
        i = max([i for i in ready[q] if max(free[q], rt[i]) <= e + EPS], key=lambda i: (bl[i], -i))
        ready[q].remove(i)
        o = ops[i]
        free[q] = max(free[q], rt[i]) + o["cost"]
        end = free[q] + o["lat"]
        if o["dma"]:
            end = dma = max(dma, free[q] + DLAT) + o["dma"] / BW
        out.append(i)
        for j in succ[i]:
            rt[j] = max(rt[j], end + HOP if ops[j]["deps"][i] else free[q])
            need[j] -= 1
            if need[j] == 0:
                ready[ops[j]["q"]].append(j)
    return out


def rank_program(g, core, T, topo):
    rank = T.rank_of(core)
    if rank is None:
        return
    ops = plan()
    seq = order(ops)
    queue = {"v": g.vector, "a": g.scalar, "p": g.tensor, "g": g, "s": g.sync}
    watched, last = [False] * len(ops), {}
    for o in ops:
        for j, must in o["deps"].items():
            watched[j] = watched[j] or must
    for i in seq:
        last[ops[i]["q"]] = i
    dsts, eng, used = [T.cores[(rank + d) % N] for d in range(1, D + 1)], {}, []
    for z in sorted(dsts, key=lambda z: len(topo.engines(core, z))):
        eng[z] = [e for e in topo.engines(core, z) if e not in used][:4]
        used = used + eng[z]
    tok, total, waited, seen, nd = {}, {}, {}, {}, 0
    for i in seq:
        o, req = ops[i], {}
        q = o["q"]
        for j, must in o["deps"].items():
            if must:
                s, v = tok[j]
                req[s] = max(req.get(s, 0), v)
        for s in sorted(req):
            if seen.get((q, s), 0) < req[s]:
                queue[q].wait_ge(T.sem[s], req[s])
                seen[(q, s)] = req[s]
                waited[s] = max(waited.get(s, 0), req[s])
        if isinstance(o["fn"], int):
            w, tr = o["fn"], []
            for d, z in enumerate(dsts):
                rid, pid, _ = topo.addr(z)
                tr.append(RemoteDMATransfer(dst_ids=[DstId(rid=rid, pnc=pid)], dma_engine_mask=sum(1 << e for e in eng[z]), remote_sem=T.sem["gh%d" % w],
                                            src=T["snd%d" % w][:, d * PW:d * PW + PW], dst=T["rcv%d" % w][:, d * PW:d * PW + PW]))
            g.remote_dma_fused(tr, local_sem=T.sem.sent)
            total["sent"] = total.get("sent", 0) + sum(len(eng[z]) for z in dsts)
            tok[i] = ("gh%d" % w, 4 * D)
            total["gh%d" % w] = 4 * D
            continue
        r = o["fn"](g, T)
        if o["dma"]:
            s, nd = "d%d" % nd, nd + 1
            r.then_inc(T.sem[s], 16)
            total[s] = 16
            tok[i] = (s, 16)
        elif watched[i] or last[q] == i:
            s = "s" + q
            total[s] = total.get(s, 0) + 1
            r.then_inc(T.sem[s], 1)
            tok[i] = (s, total[s])
    for s in total:
        if waited.get(s, 0) < total[s]:
            g.wait_ge(T.sem[s], total[s])
